import numpy as np
import ml_dtypes


def mxq(x, axis, fmt="e4m3"):
    dtype, down = {"e4m3": (ml_dtypes.float8_e4m3fn, 7), "e5m2": (ml_dtypes.float8_e5m2, 14)}[fmt]
    v = np.moveaxis(np.asarray(x, np.float32).astype(ml_dtypes.bfloat16).astype(np.float64), axis, -1)
    blocks = v.reshape(v.shape[:-1] + (-1, 32))
    amax = np.abs(blocks).max(-1, keepdims=True)
    byte = np.maximum(np.where(amax > 0, np.frexp(amax)[1] - 1 + 127, 0) - down, 1)
    scale = np.exp2(byte - 127.0)
    codes = (blocks / scale).astype(np.float32).astype(dtype).astype(np.float64)
    return np.moveaxis((codes * scale).reshape(v.shape), -1, axis)


WIDE = False


def mx_kscale(k):
    if not WIDE:
        return np.ones(k)
    levels = np.array([10, -10, 5, -5, 0])
    if k % 512:
        return np.exp2(np.random.permutation(np.resize(levels, k // 32))).repeat(32)
    a = np.empty((k // 512, 16))
    for p in range(k // 512):
        a[p, :8] = np.random.permutation(np.resize(levels, 8))
        for g in range(8):
            far = levels[np.abs(levels - a[p, g]) >= 10]
            a[p, g + 8] = far[np.random.randint(len(far))]
    return np.exp2(a.ravel()).repeat(32)


def f64(x):
    return np.asarray(x).astype(np.float64)


def striped(idx):
    return np.tile(np.asarray(idx).reshape(-1, 16).T, (8, 1)).astype(np.uint16)


def unstriped(offs):
    return offs[:16].T.reshape(-1).astype(np.int64)


E2M1 = np.array([0.0, 0.5, 1.0, 1.5, 2.0, 3.0, 4.0, 6.0, -0.0, -0.5, -1.0, -1.5, -2.0, -3.0, -4.0, -6.0])


def pack_weight(w, fmt):
    k, n = w.shape
    w = f64(np.asarray(w, np.float32).astype(ml_dtypes.bfloat16)).reshape(k // 32, 32, n)
    amax = np.abs(w).max(1)
    if fmt == "e4m3":
        byte = np.frexp(amax)[1] - 1 + 127 - 7
    else:
        mant, ex = np.frexp(amax / 6.0)
        byte = np.where(mant > 0.5, ex, ex - 1) + 127
    byte = np.clip(np.where(amax > 0, byte, 1), 1, 254)
    scaled = (w * np.exp2(127.0 - byte)[:, None, :]).reshape(k, n).astype(np.float32)
    by_word = np.ascontiguousarray(scaled.reshape(k // 512, 128, 4, n).transpose(0, 1, 3, 2))
    if fmt == "e4m3":
        words = by_word.astype(ml_dtypes.float8_e4m3fn).view(np.uint8)
    else:
        c = by_word.astype(ml_dtypes.float4_e2m1fn).view(np.uint8) & 0xF
        words = (c[..., 0::2] | (c[..., 1::2] << 4)).reshape(k // 512, 128, 2 * n)
    return np.ascontiguousarray(words), np.ascontiguousarray(byte.astype(np.uint8).reshape(k // 512, 16, n))


def unpack_weight(words, scales, fmt):
    g, _, n = scales.shape
    words = np.ascontiguousarray(words).reshape(g, 128, n, -1)
    if fmt == "e4m3":
        vals = words.view(ml_dtypes.float8_e4m3fn).astype(np.float64)
    else:
        nib = np.empty((g, 128, n, 4), np.uint8)
        nib[..., 0::2] = words & 0xF
        nib[..., 1::2] = words >> 4
        vals = E2M1[nib]
    vals = vals * np.repeat(np.exp2(scales.astype(np.float64) - 127.0), 8, axis=1)[..., None]
    return vals.transpose(0, 1, 3, 2).reshape(g * 512, n)


def bf(x):
    return np.asarray(x, np.float32).astype(ml_dtypes.bfloat16)


def planes(Y):
    r, m = Y.shape
    b = f64(bf(Y)).reshape(r // 32, 32, m)
    amax = np.abs(b).max(1)
    byte = np.clip(np.where(amax > 0, np.frexp(amax)[1] - 1 + 127 - 7, 1), 1, 254)
    codes = (b * np.exp2(127.0 - byte)[:, None, :]).reshape(r, m).astype(np.float32).astype(ml_dtypes.float8_e4m3fn).view(np.uint8)
    words = codes.reshape(r // 512, 128, 4, m).transpose(0, 1, 3, 2)
    return np.ascontiguousarray(words), np.ascontiguousarray(byte.astype(np.uint8).reshape(r // 512, 16, m))


D, T, I, J, Q = 512, 2048, 512, 256, 512


def setup_inputs():
    n = np.random.standard_normal
    idx = np.random.permutation(T)[:I]
    idx2 = np.random.permutation(T)[:J]
    fd = mx_kscale(D)
    keysp = pack_weight(n((D, T)) / fd[:, None], "e4m3")
    return {
        "query": (n((D, Q)) * 0.6 / np.sqrt(D) * fd[:, None]).astype(np.float32),
        "keys_words": keysp[0],
        "keys_scales": keysp[1],
        "mass": (np.random.uniform(0.0, 2.0, (Q, T))).astype(np.float32),
        "dec": (np.random.uniform(0.8, 1.0, (Q, 1))).astype(np.float32),
        "credit": (np.random.uniform(0.0, 0.5, (1, T))).astype(np.float32),
        "offs": striped(idx),
        "offs2": striped(idx2),
    }


def reference(query, keys_words, keys_scales, mass, dec, credit, offs, offs2):
    idx = unstriped(offs)
    idx2 = unstriped(offs2)
    keysu = unpack_weight(keys_words, keys_scales, "e4m3")
    queryq = mxq(f64(query), 0, "e4m3")
    keysidxg = keysu[:, idx]
    a = queryq.T @ keysidxg
    p = np.exp(a - np.max(a, axis=1, keepdims=True))
    w = p / np.sum(p, axis=1, keepdims=True) * 512.0
    wf = np.zeros((Q, T))
    wf[:, idx] = w
    x = f64(dec) * f64(mass) + wf - f64(credit)
    y = x[:, idx2] * 2.0
    words, scales = planes(y)
    return y, words, scales

@@ -1,0 +1,242 @@
+from contextlib import ExitStack
+
+import concourse.mybir as mybir
+from concourse.masks import make_identity
+
+D, T, I, J, Q = 512, 2048, 512, 256, 512
+FLOPS = 2 * D * Q * I
+
+F32 = mybir.dt.float32
+BF16 = mybir.dt.bfloat16
+I32 = mybir.dt.int32
+U32 = mybir.dt.uint32
+U16 = mybir.dt.uint16
+U8 = mybir.dt.uint8
+FP8X4 = mybir.dt.float8_e4m3fn_x4
+ACT = mybir.ActivationFunctionType
+ALU = mybir.AluOpType
+AX = mybir.AxisListType
+
+P = 128
+PACK = 4
+CHUNK = 512
+CHUNKS = T // CHUNK
+BLOCKS = CHUNK // P
+WINDOWS = 3
+M_VECTOR = 80
+SCALAR_CHUNKS = (3, 3, 0, 0)
+TURNED_CHUNKS = (3, 3, 3, 3)
+
+
+def tile_attend_evictscores_pl_kernel(tc, query, keys_words, keys_scales, mass, dec, credit, offs, offs2, out_0, out_1, out_2):
+    nc = tc.nc
+    with ExitStack() as ctx:
+        keep = ctx.enter_context(tc.tile_pool(name="keep", bufs=1))
+        ring = ctx.enter_context(tc.tile_pool(name="ring", bufs=4))
+        psum = ctx.enter_context(tc.psum_pool(name="psum", bufs=1))
+
+        slots = keep.tile([P, I // 16], U16, name="slots")
+        nc.sync.dma_start(slots[:], offs)
+        cands = keep.tile([P, J // 16], U16, name="cands")
+        nc.sync.dma_start(cands[:], offs2)
+        q_raw = keep.tile([P, PACK, Q], F32, name="q_raw", tag="first")
+        nc.sync.dma_start(q_raw[:], query.rearrange("(p j) c -> p j c", j=PACK))
+        k_words = keep.tile([P, T], U32, name="k_words", tag="words")
+        nc.sync.dma_start(k_words[:].bitcast(I32), keys_words[0].rearrange("p c r -> p (c r)").bitcast(I32))
+
+        k_scales = keep.tile([P, T], U8, name="k_scales", tag="rest")
+        nc.vector.memset(k_scales[:].bitcast(I32), 0)
+        for quad in range(4):
+            nc.scalar.dma_start(k_scales[32 * quad : 32 * quad + 4, :].bitcast(I32), keys_scales[0, 4 * quad : 4 * quad + 4, :].bitcast(I32))
+
+        ident = keep.tile([P, P], F32, name="ident")
+        credit_rows = keep.tile([P, P], F32, name="credit_rows")
+        nc.gpsimd.memset(credit_rows[:], 0.0)
+        nc.gpsimd.dma_start(credit_rows[0 : T // P, :], credit.rearrange("o (b m) -> (o b) m", m=P))
+        dec_cols = keep.tile([P, PACK], F32, name="dec_cols")
+        nc.gpsimd.dma_start(dec_cols[:], dec.rearrange("(p t) o -> p (t o)", t=PACK))
+        make_identity(nc, ident[:])
+
+        windows = [keep.tile([P, T], F32, name="window%d" % i) for i in range(WINDOWS)]
+        for window in windows:
+            nc.vector.memset(window[:], 0.0)
+
+        kg_scales = keep.tile([P, I], U8, name="kg_scales", align_bytes=64)
+        nc.vector.tensor_copy(kg_scales[:], k_scales[:].indirect(slots[:]))
+
+        q_bf = keep.tile([P, PACK * Q], BF16, name="q_bf", align_bytes=64)
+        q_dst = q_bf[:].rearrange("p (t m j) -> p m j t", t=PACK, j=PACK)
+        q_src = q_raw[:].rearrange("p j (m t) -> p m j t", t=PACK)
+        nc.vector.tensor_copy(q_dst[:, :M_VECTOR], q_src[:, :M_VECTOR])
+        nc.scalar.copy(q_dst[:, M_VECTOR:], q_src[:, M_VECTOR:])
+        q_words = keep.tile([P, Q], U32, name="q_words", align_bytes=64)
+        q_scales = keep.tile([P, Q], U8, name="q_scales", align_bytes=64)
+        nc.vector.quantize_mx(out=q_words[:].bitcast(FP8X4), scales=q_scales[:], in_=q_bf[:])
+
+        kg_words = keep.tile([P, I], U32, name="kg_words", align_bytes=64)
+        nc.vector.tensor_copy(kg_words[:], k_words[:].indirect(slots[:]))
+
+        mass_rows = mass.rearrange("(p t) c -> p t c", t=PACK)
+        mass_first = keep.tile([P, T], F32, name="mass_first", tag="rest")
+        nc.sync.dma_start(mass_first[:], mass_rows[:, 0, :])
+        mass_rest = keep.tile([P, PACK - 1, T], F32, name="mass_rest", tag="first")
+        for t in range(1, PACK):
+            nc.sync.dma_start(mass_rest[:, t - 1, :], mass_rows[:, t, :])
+        spread_from = min(TURNED_CHUNKS) * CHUNK
+        credit_spread = keep.tile([P, T - spread_from], F32, name="credit_spread", tag="words")
+        nc.sync.dma_start(credit_spread[:], credit[0, spread_from:].partition_broadcast(P))
+        mass_of = [mass_first[:]] + [mass_rest[:, t, :] for t in range(PACK - 1)]
+
+        turned = psum.tile([P, CHUNK], F32, name="turned", tag="turned", bufs=4)
+        nc.tensor.transpose(turned[:, :P], credit_rows[:], ident[:])
+        credit_cols = keep.tile([P, T // P], F32, name="credit_cols")
+        nc.scalar.copy(credit_cols[:], turned[:, : T // P])
+
+        scores = [psum.tile([P, I], F32, name="scores%d" % t, tag="upright", bufs=4) for t in range(PACK)]
+        for t in range(PACK):
+            heads = slice(t * P, (t + 1) * P)
+            nc.tensor.matmul_mx(
+                out=scores[t][:],
+                lhsT=q_words[:, heads].bitcast(FP8X4),
+                lhsT_scale=q_scales[:, heads],
+                rhs=kg_words[:].bitcast(FP8X4),
+                rhs_scale=kg_scales[:],
+                start=True,
+                stop=True,
+            )
+        neg_max = keep.tile([P, PACK], F32, name="neg_max")
+        sums = keep.tile([P, PACK], F32, name="sums")
+        means = keep.tile([P, PACK], F32, name="means")
+        gains = keep.tile([P, PACK], F32, name="gains")
+        probs = [keep.tile([P, I], F32, name="probs%d" % t) for t in range(PACK)]
+        weights = [keep.tile([P, I], F32, name="weights%d" % t) for t in range(PACK)]
+        for t in range(PACK):
+            nc.vector.tensor_reduce(neg_max[:, t : t + 1], scores[t][:], AX.X, ALU.max, negate=True)
+
+        def exponentiate(t):
+            nc.scalar.activation(probs[t][:], scores[t][:], ACT.Exp, bias=neg_max[:, t : t + 1], accum_out=sums[:, t : t + 1])
+
+        def invert(lo, hi):
+            nc.scalar.activation(means[:, lo:hi], sums[:, lo:hi], ACT.Copy, scale=1.0 / I)
+            nc.vector.reciprocal(gains[:, lo:hi], means[:, lo:hi])
+
+        def normalise(t):
+            nc.scalar.activation(weights[t][:], probs[t][:], ACT.Copy, scale=gains[:, t : t + 1])
+
+        exponentiate(0)
+        invert(0, 1)
+        exponentiate(1)
+        invert(1, 2)
+        normalise(0)
+        exponentiate(2)
+        exponentiate(3)
+        invert(2, 4)
+        decayed = {}
+
+        def decay(t):
+            width = SCALAR_CHUNKS[t] * CHUNK
+            decayed[t] = keep.tile([P, width], F32, name="decayed%d" % t)
+            nc.scalar.activation(decayed[t][:], mass_of[t][:, :width], ACT.Copy, scale=dec_cols[:, t : t + 1])
+
+        normalise(1)
+        decay(0)
+        normalise(2)
+        normalise(3)
+
+        def scatter(t):
+            nc.vector.tensor_copy(windows[t % WINDOWS][:].indirect(slots[:]), weights[t][:])
+
+        updated = [keep.tile([P, T], F32, name="updated%d" % t) for t in range(PACK)]
+        picked = keep.tile([P, PACK, J], F32, name="picked")
+        out_rows = out_0.rearrange("(p t) j -> p t j", t=PACK)
+
+        blocks = [slice(b * P, (b + 1) * P) for b in range(BLOCKS)]
+
+        def turn(t, c):
+            cols = slice(c * CHUNK, (c + 1) * CHUNK)
+            turned = psum.tile([P, CHUNK], F32, name="turned", tag="turned", bufs=4)
+            terms = [decayed[t][:, cols]] if c < SCALAR_CHUNKS[t] else []
+            terms.append(windows[t % WINDOWS][:, cols])
+            for i, term in enumerate(terms):
+                for b, block in enumerate(blocks):
+                    first = i == 0 and b == 0
+                    last = i == len(terms) - 1 and b == BLOCKS - 1
+                    nc.tensor.matmul(turned[:, block], term[:, block], ident[:], start=first, stop=last, is_transpose=True)
+            return turned
+
+        def charge(c, turned):
+            owed = ring.tile([P, CHUNK], F32, name="owed")
+            for b, block in enumerate(blocks):
+                k = c * BLOCKS + b
+                nc.scalar.activation(owed[:, block], turned[:, block], ACT.Identity, scale=-1.0, bias=credit_cols[:, k : k + 1])
+            return owed
+
+        def turn_back(owed):
+            upright = psum.tile([P, CHUNK], F32, name="upright", tag="upright", bufs=4)
+            for block in blocks:
+                nc.tensor.transpose(upright[:, block], owed[:, block], ident[:])
+            return upright
+
+        def finish(t, c, upright):
+            cols = slice(c * CHUNK, (c + 1) * CHUNK)
+            if c < SCALAR_CHUNKS[t]:
+                nc.scalar.activation(updated[t][:, cols], upright[:], ACT.Copy, scale=-1.0)
+            else:
+                nc.vector.scalar_tensor_tensor(updated[t][:, cols], mass_of[t][:, cols], dec_cols[:, t : t + 1], upright[:], ALU.mult, ALU.subtract)
+
+        def update_plain(t):
+            first = TURNED_CHUNKS[t] * CHUNK
+            nc.vector.scalar_tensor_tensor(
+                updated[t][:, first:], mass_of[t][:, first:], dec_cols[:, t : t + 1], credit_spread[:, first - spread_from :], ALU.mult, ALU.subtract
+            )
+            nc.vector.tensor_tensor(updated[t][:, first:], updated[t][:, first:], windows[t % WINDOWS][:, first:], ALU.add)
+
+        def look_up(t):
+            nc.vector.tensor_copy(picked[:, t, :], updated[t][:].indirect(cands[:]))
+            doubled = keep.tile([P, J], F32, name="doubled%d" % t)
+            nc.scalar.activation(doubled[:], picked[:, t, :], ACT.Copy, scale=2.0)
+            nc.sync.dma_start(out_rows[:, t, :], doubled[:])
+
+        for t in range(WINDOWS):
+            scatter(t)
+        work = [(t, c) for t in range(PACK) for c in range(TURNED_CHUNKS[t])]
+        turned_of, owed_of, upright_of = {}, {}, {}
+        for step in range(len(work) + 3):
+            if step < len(work):
+                t, c = work[step]
+                if c == 0 and t > 0 and SCALAR_CHUNKS[t]:
+                    decay(t)
+                turned_of[step] = turn(t, c)
+                if c == TURNED_CHUNKS[t] - 1:
+                    if TURNED_CHUNKS[t] < CHUNKS:
+                        update_plain(t)
+                    if t + WINDOWS < PACK:
+                        scatter(t + WINDOWS)
+            n = step - 1
+            if 0 <= n < len(work):
+                owed_of[n] = charge(work[n][1], turned_of[n])
+            n = step - 2
+            if 0 <= n < len(work):
+                upright_of[n] = turn_back(owed_of[n])
+            n = step - 3
+            if 0 <= n < len(work):
+                t, c = work[n]
+                finish(t, c, upright_of[n])
+                if c == TURNED_CHUNKS[t] - 1:
+                    look_up(t)
+
+        y_bf = keep.tile([P, J * PACK], BF16, name="y_bf", align_bytes=64)
+        nc.vector.tensor_scalar(
+            y_bf[:].rearrange("p (c i t) -> p c t i", i=4, t=PACK),
+            picked[:].rearrange("p t (c i) -> p c t i", i=4),
+            2.0,
+            None,
+            ALU.mult,
+        )
+        y_words = keep.tile([P, J], U32, name="y_words", align_bytes=64)
+        y_scales = keep.tile([P, J], U8, name="y_scales", align_bytes=64)
+        nc.vector.quantize_mx(out=y_words[:].bitcast(FP8X4), scales=y_scales[:], in_=y_bf[:])
+        nc.sync.dma_start(out_1[0].rearrange("p c r -> p (c r)").bitcast(I32), y_words[:].bitcast(I32))
+        for quad in range(4):
+            queue = nc.scalar if quad % 2 == 0 else nc.sync
+            queue.dma_start(out_2[0, 4 * quad : 4 * quad + 4, :].bitcast(I32), y_scales[32 * quad : 32 * quad + 4, :].bitcast(I32))

@@ -20,12 +20,11 @@ AX = mybir.AxisListType
 P = 128
 PACK = 4
 CHUNK = 512
-CHUNKS = T // CHUNK
 BLOCKS = CHUNK // P
+LEFT = 1024
 WINDOWS = 3
-M_VECTOR = 80
-SCALAR_CHUNKS = (3, 3, 0, 0)
-TURNED_CHUNKS = (3, 3, 3, 3)
+VECTOR_CHUNKS = (0, 0, 1, 2)
+GPSIMD_DECAYS = (0, 1,)
 
 
 def tile_attend_evictscores_pl_kernel(tc, query, keys_words, keys_scales, mass, dec, credit, offs, offs2, out_0, out_1, out_2):
@@ -34,6 +33,9 @@ def tile_attend_evictscores_pl_kernel(tc, query, keys_words, keys_scales, mass, 
         keep = ctx.enter_context(tc.tile_pool(name="keep", bufs=1))
         ring = ctx.enter_context(tc.tile_pool(name="ring", bufs=4))
         psum = ctx.enter_context(tc.psum_pool(name="psum", bufs=1))
+
+        def bank(name, b):
+            return psum.tile([P, CHUNK], F32, name=name, tag="bank%d" % b)
 
         slots = keep.tile([P, I // 16], U16, name="slots")
         nc.sync.dma_start(slots[:], offs)
@@ -44,59 +46,80 @@ def tile_attend_evictscores_pl_kernel(tc, query, keys_words, keys_scales, mass, 
         k_words = keep.tile([P, T], U32, name="k_words", tag="words")
         nc.sync.dma_start(k_words[:].bitcast(I32), keys_words[0].rearrange("p c r -> p (c r)").bitcast(I32))
 
+        mass_rows = mass.rearrange("(p t) c -> p t c", t=PACK)
+        mass_right = keep.tile([P, T - LEFT], F32, name="mass_right")
+        nc.sync.dma_start(mass_right[:], mass_rows[:, 0, LEFT:])
+
         k_scales = keep.tile([P, T], U8, name="k_scales", tag="rest")
         nc.vector.memset(k_scales[:].bitcast(I32), 0)
         for quad in range(4):
             nc.scalar.dma_start(k_scales[32 * quad : 32 * quad + 4, :].bitcast(I32), keys_scales[0, 4 * quad : 4 * quad + 4, :].bitcast(I32))
 
-        ident = keep.tile([P, P], F32, name="ident")
         credit_rows = keep.tile([P, P], F32, name="credit_rows")
         nc.gpsimd.memset(credit_rows[:], 0.0)
-        nc.gpsimd.dma_start(credit_rows[0 : T // P, :], credit.rearrange("o (b m) -> (o b) m", m=P))
-        dec_cols = keep.tile([P, PACK], F32, name="dec_cols")
-        nc.gpsimd.dma_start(dec_cols[:], dec.rearrange("(p t) o -> p (t o)", t=PACK))
-        make_identity(nc, ident[:])
+        nc.scalar.dma_start(credit_rows[0 : LEFT // P, :], credit[:, :LEFT].rearrange("o (b m) -> (o b) m", m=P))
 
-        windows = [keep.tile([P, T], F32, name="window%d" % i) for i in range(WINDOWS)]
+        ident = keep.tile([P, P], F32, name="ident")
+        make_identity(nc, ident[:])
+        windows = [keep.tile([P, T], F32, name="window%d" % i) for i in range(WINDOWS - 1)]
         for window in windows:
             nc.vector.memset(window[:], 0.0)
 
-        kg_scales = keep.tile([P, I], U8, name="kg_scales", align_bytes=64)
-        nc.vector.tensor_copy(kg_scales[:], k_scales[:].indirect(slots[:]))
-
-        q_bf = keep.tile([P, PACK * Q], BF16, name="q_bf", align_bytes=64)
-        q_dst = q_bf[:].rearrange("p (t m j) -> p m j t", t=PACK, j=PACK)
-        q_src = q_raw[:].rearrange("p j (m t) -> p m j t", t=PACK)
-        nc.vector.tensor_copy(q_dst[:, :M_VECTOR], q_src[:, :M_VECTOR])
-        nc.scalar.copy(q_dst[:, M_VECTOR:], q_src[:, M_VECTOR:])
+        q_bf = keep.tile([P, PACK, P * PACK], BF16, name="q_bf", align_bytes=64)
+        q_src = q_raw[:].rearrange("p j (m t) -> p t m j", t=PACK)
         q_words = keep.tile([P, Q], U32, name="q_words", align_bytes=64)
         q_scales = keep.tile([P, Q], U8, name="q_scales", align_bytes=64)
-        nc.vector.quantize_mx(out=q_words[:].bitcast(FP8X4), scales=q_scales[:], in_=q_bf[:])
 
+        def quantise(lo, hi):
+            heads = slice(lo * P, hi * P)
+            nc.vector.quantize_mx(out=q_words[:, heads].bitcast(FP8X4), scales=q_scales[:, heads], in_=q_bf[:, lo:hi, :].rearrange("p t k -> p (t k)"))
+
+        nc.vector.tensor_copy(q_bf[:, 0, :].rearrange("p (m j) -> p m j", j=PACK), q_src[:, 0])
+        for t in range(1, PACK):
+            nc.scalar.copy(q_bf[:, t, :].rearrange("p (m j) -> p m j", j=PACK), q_src[:, t])
+        quantise(0, 1)
+        kg_scales = keep.tile([P, I], U8, name="kg_scales", align_bytes=64)
+        nc.vector.tensor_copy(kg_scales[:], k_scales[:].indirect(slots[:]))
         kg_words = keep.tile([P, I], U32, name="kg_words", align_bytes=64)
         nc.vector.tensor_copy(kg_words[:], k_words[:].indirect(slots[:]))
+        quantise(1, 2)
+        quantise(2, 4)
+        windows.append(keep.tile([P, T], F32, name="window_late", tag="words"))
+        nc.gpsimd.memset(windows[-1][:], 0.0)
 
-        mass_rows = mass.rearrange("(p t) c -> p t c", t=PACK)
-        mass_first = keep.tile([P, T], F32, name="mass_first", tag="rest")
-        nc.sync.dma_start(mass_first[:], mass_rows[:, 0, :])
+        early = keep.tile([P, T + 8], F32, name="early", tag="rest")
+        mass_left = early[:, :LEFT]
+        credit_spread = early[:, LEFT:T]
+        dec_cols = early[:, T : T + PACK]
+        nc.sync.dma_start(dec_cols, dec.rearrange("(p t) o -> p (t o)", t=PACK))
+        nc.sync.dma_start(credit_spread, credit[0, LEFT:].partition_broadcast(P))
+        nc.sync.dma_start(mass_left, mass_rows[:, 0, :LEFT])
         mass_rest = keep.tile([P, PACK - 1, T], F32, name="mass_rest", tag="first")
         for t in range(1, PACK):
             nc.sync.dma_start(mass_rest[:, t - 1, :], mass_rows[:, t, :])
-        spread_from = min(TURNED_CHUNKS) * CHUNK
-        credit_spread = keep.tile([P, T - spread_from], F32, name="credit_spread", tag="words")
-        nc.sync.dma_start(credit_spread[:], credit[0, spread_from:].partition_broadcast(P))
-        mass_of = [mass_first[:]] + [mass_rest[:, t, :] for t in range(PACK - 1)]
 
-        turned = psum.tile([P, CHUNK], F32, name="turned", tag="turned", bufs=4)
-        nc.tensor.transpose(turned[:, :P], credit_rows[:], ident[:])
-        credit_cols = keep.tile([P, T // P], F32, name="credit_cols")
-        nc.scalar.copy(credit_cols[:], turned[:, : T // P])
+        def mass_cols(t, lo, hi):
+            if t > 0:
+                return mass_rest[:, t - 1, lo:hi]
+            return mass_left[:, lo:hi] if hi <= LEFT else mass_right[:, lo - LEFT : hi - LEFT]
 
-        scores = [psum.tile([P, I], F32, name="scores%d" % t, tag="upright", bufs=4) for t in range(PACK)]
-        for t in range(PACK):
+        credit_turned = bank("credit_turned", 3)
+        nc.tensor.transpose(credit_turned[:, :P], credit_rows[:], ident[:])
+        credit_cols = keep.tile([P, LEFT // P], F32, name="credit_cols")
+        nc.scalar.copy(credit_cols[:], credit_turned[:, : LEFT // P])
+
+        neg_max = keep.tile([P, PACK], F32, name="neg_max")
+        sums = keep.tile([P, PACK], F32, name="sums")
+        inverses = keep.tile([P, PACK], F32, name="inverses")
+        gains = keep.tile([P, PACK], F32, name="gains")
+        probs = [keep.tile([P, I], F32, name="probs%d" % t) for t in range(PACK)]
+        weights = [keep.tile([P, I], F32, name="weights%d" % t) for t in range(PACK)]
+
+        def exponentiate(t):
             heads = slice(t * P, (t + 1) * P)
+            scores = bank("scores", t % 3)
             nc.tensor.matmul_mx(
-                out=scores[t][:],
+                out=scores[:],
                 lhsT=q_words[:, heads].bitcast(FP8X4),
                 lhsT_scale=q_scales[:, heads],
                 rhs=kg_words[:].bitcast(FP8X4),
@@ -104,42 +127,36 @@ def tile_attend_evictscores_pl_kernel(tc, query, keys_words, keys_scales, mass, 
                 start=True,
                 stop=True,
             )
-        neg_max = keep.tile([P, PACK], F32, name="neg_max")
-        sums = keep.tile([P, PACK], F32, name="sums")
-        means = keep.tile([P, PACK], F32, name="means")
-        gains = keep.tile([P, PACK], F32, name="gains")
-        probs = [keep.tile([P, I], F32, name="probs%d" % t) for t in range(PACK)]
-        weights = [keep.tile([P, I], F32, name="weights%d" % t) for t in range(PACK)]
-        for t in range(PACK):
-            nc.vector.tensor_reduce(neg_max[:, t : t + 1], scores[t][:], AX.X, ALU.max, negate=True)
-
-        def exponentiate(t):
-            nc.scalar.activation(probs[t][:], scores[t][:], ACT.Exp, bias=neg_max[:, t : t + 1], accum_out=sums[:, t : t + 1])
+            nc.vector.tensor_reduce(neg_max[:, t : t + 1], scores[:], AX.X, ALU.max, negate=True)
+            nc.scalar.activation(probs[t][:], scores[:], ACT.Exp, bias=neg_max[:, t : t + 1], accum_out=sums[:, t : t + 1])
 
         def invert(lo, hi):
-            nc.scalar.activation(means[:, lo:hi], sums[:, lo:hi], ACT.Copy, scale=1.0 / I)
-            nc.vector.reciprocal(gains[:, lo:hi], means[:, lo:hi])
+            nc.vector.reciprocal(inverses[:, lo:hi], sums[:, lo:hi])
+            if lo == 0:
+                nc.vector.tensor_scalar(gains[:, lo:hi], inverses[:, lo:hi], float(I), None, ALU.mult)
+            else:
+                nc.scalar.activation(gains[:, lo:hi], inverses[:, lo:hi], ACT.Copy, scale=float(I))
 
         def normalise(t):
             nc.scalar.activation(weights[t][:], probs[t][:], ACT.Copy, scale=gains[:, t : t + 1])
 
+        decayed = [keep.tile([P, T], F32, name="decayed%d" % t) for t in range(PACK)]
+
+        def decay_on_scalar(t):
+            lo = VECTOR_CHUNKS[t] * CHUNK
+            hi = LEFT if t in GPSIMD_DECAYS else T
+            nc.scalar.activation(decayed[t][:, lo:hi], mass_cols(t, lo, hi), ACT.Copy, scale=dec_cols[:, t : t + 1])
+
         exponentiate(0)
         invert(0, 1)
         exponentiate(1)
-        invert(1, 2)
         normalise(0)
+        invert(1, 2)
         exponentiate(2)
         exponentiate(3)
-        invert(2, 4)
-        decayed = {}
-
-        def decay(t):
-            width = SCALAR_CHUNKS[t] * CHUNK
-            decayed[t] = keep.tile([P, width], F32, name="decayed%d" % t)
-            nc.scalar.activation(decayed[t][:], mass_of[t][:, :width], ACT.Copy, scale=dec_cols[:, t : t + 1])
-
         normalise(1)
-        decay(0)
+        decay_on_scalar(0)
+        invert(2, 4)
         normalise(2)
         normalise(3)
 
@@ -149,13 +166,21 @@ def tile_attend_evictscores_pl_kernel(tc, query, keys_words, keys_scales, mass, 
         updated = [keep.tile([P, T], F32, name="updated%d" % t) for t in range(PACK)]
         picked = keep.tile([P, PACK, J], F32, name="picked")
         out_rows = out_0.rearrange("(p t) j -> p t j", t=PACK)
-
         blocks = [slice(b * P, (b + 1) * P) for b in range(BLOCKS)]
 
-        def turn(t, c):
+        def charge_right(t):
+            if t in GPSIMD_DECAYS:
+                nc.gpsimd.tensor_scalar(decayed[t][:, LEFT:], mass_cols(t, LEFT, T), dec_cols[:, t : t + 1], 0.0, ALU.mult, ALU.add)
+            nc.gpsimd.tensor_tensor(updated[t][:, LEFT:], decayed[t][:, LEFT:], credit_spread, ALU.subtract)
+
+        def add_right(t):
+            engine = nc.vector if t == PACK - 1 else nc.gpsimd
+            engine.tensor_tensor(updated[t][:, LEFT:], updated[t][:, LEFT:], windows[t % WINDOWS][:, LEFT:], ALU.add)
+
+        def turn(n, t, c):
             cols = slice(c * CHUNK, (c + 1) * CHUNK)
-            turned = psum.tile([P, CHUNK], F32, name="turned", tag="turned", bufs=4)
-            terms = [decayed[t][:, cols]] if c < SCALAR_CHUNKS[t] else []
+            turned = bank("turned", 3 + n % 3)
+            terms = [decayed[t][:, cols]] if c >= VECTOR_CHUNKS[t] else []
             terms.append(windows[t % WINDOWS][:, cols])
             for i, term in enumerate(terms):
                 for b, block in enumerate(blocks):
@@ -164,32 +189,25 @@ def tile_attend_evictscores_pl_kernel(tc, query, keys_words, keys_scales, mass, 
                     nc.tensor.matmul(turned[:, block], term[:, block], ident[:], start=first, stop=last, is_transpose=True)
             return turned
 
-        def charge(c, turned):
+        def charge_left(c, turned):
             owed = ring.tile([P, CHUNK], F32, name="owed")
             for b, block in enumerate(blocks):
                 k = c * BLOCKS + b
                 nc.scalar.activation(owed[:, block], turned[:, block], ACT.Identity, scale=-1.0, bias=credit_cols[:, k : k + 1])
             return owed
 
-        def turn_back(owed):
-            upright = psum.tile([P, CHUNK], F32, name="upright", tag="upright", bufs=4)
+        def turn_back(n, owed):
+            upright = bank("upright", (6, 7, 0, 1, 2)[n % 5])
             for block in blocks:
                 nc.tensor.transpose(upright[:, block], owed[:, block], ident[:])
             return upright
 
         def finish(t, c, upright):
             cols = slice(c * CHUNK, (c + 1) * CHUNK)
-            if c < SCALAR_CHUNKS[t]:
+            if c >= VECTOR_CHUNKS[t]:
                 nc.scalar.activation(updated[t][:, cols], upright[:], ACT.Copy, scale=-1.0)
             else:
-                nc.vector.scalar_tensor_tensor(updated[t][:, cols], mass_of[t][:, cols], dec_cols[:, t : t + 1], upright[:], ALU.mult, ALU.subtract)
-
-        def update_plain(t):
-            first = TURNED_CHUNKS[t] * CHUNK
-            nc.vector.scalar_tensor_tensor(
-                updated[t][:, first:], mass_of[t][:, first:], dec_cols[:, t : t + 1], credit_spread[:, first - spread_from :], ALU.mult, ALU.subtract
-            )
-            nc.vector.tensor_tensor(updated[t][:, first:], updated[t][:, first:], windows[t % WINDOWS][:, first:], ALU.add)
+                nc.vector.scalar_tensor_tensor(updated[t][:, cols], mass_cols(t, c * CHUNK, (c + 1) * CHUNK), dec_cols[:, t : t + 1], upright[:], ALU.mult, ALU.subtract)
 
         def look_up(t):
             nc.vector.tensor_copy(picked[:, t, :], updated[t][:].indirect(cands[:]))
@@ -199,30 +217,37 @@ def tile_attend_evictscores_pl_kernel(tc, query, keys_words, keys_scales, mass, 
 
         for t in range(WINDOWS):
             scatter(t)
-        work = [(t, c) for t in range(PACK) for c in range(TURNED_CHUNKS[t])]
+        charge_right(0)
+        charge_right(1)
+        work = [(t, c) for t in range(PACK) for c in reversed(range(LEFT // CHUNK))]
         turned_of, owed_of, upright_of = {}, {}, {}
         for step in range(len(work) + 3):
             if step < len(work):
                 t, c = work[step]
-                if c == 0 and t > 0 and SCALAR_CHUNKS[t]:
-                    decay(t)
-                turned_of[step] = turn(t, c)
-                if c == TURNED_CHUNKS[t] - 1:
-                    if TURNED_CHUNKS[t] < CHUNKS:
-                        update_plain(t)
+                turned_of[step] = turn(step, t, c)
+                if c == 0:
+                    if t == 0:
+                        decay_on_scalar(1)
+                    if t == 1:
+                        decay_on_scalar(2)
+                        decay_on_scalar(3)
+                    add_right(t)
+                    if t == 1:
+                        charge_right(2)
+                        charge_right(3)
                     if t + WINDOWS < PACK:
                         scatter(t + WINDOWS)
             n = step - 1
             if 0 <= n < len(work):
-                owed_of[n] = charge(work[n][1], turned_of[n])
+                owed_of[n] = charge_left(work[n][1], turned_of[n])
             n = step - 2
             if 0 <= n < len(work):
-                upright_of[n] = turn_back(owed_of[n])
+                upright_of[n] = turn_back(n, owed_of[n])
             n = step - 3
             if 0 <= n < len(work):
                 t, c = work[n]
                 finish(t, c, upright_of[n])
-                if c == TURNED_CHUNKS[t] - 1:
+                if c == 0:
                     look_up(t)
 
         y_bf = keep.tile([P, J * PACK], BF16, name="y_bf", align_bytes=64)

@@ -23,7 +23,7 @@ CHUNK = 512
 BLOCKS = CHUNK // P
 LEFT = 1024
 WINDOWS = 3
-VECTOR_CHUNKS = (0, 0, 1, 2)
+VECTOR_CHUNKS = (0, 0, 0, 2)
 GPSIMD_DECAYS = (0, 1,)
 
 
@@ -43,12 +43,12 @@ def tile_attend_evictscores_pl_kernel(tc, query, keys_words, keys_scales, mass, 
         nc.sync.dma_start(cands[:], offs2)
         q_raw = keep.tile([P, PACK, Q], F32, name="q_raw", tag="first")
         nc.sync.dma_start(q_raw[:], query.rearrange("(p j) c -> p j c", j=PACK))
-        k_words = keep.tile([P, T], U32, name="k_words", tag="words")
+        k_words = keep.tile([P, T], U32, name="k_words")
         nc.sync.dma_start(k_words[:].bitcast(I32), keys_words[0].rearrange("p c r -> p (c r)").bitcast(I32))
 
         mass_rows = mass.rearrange("(p t) c -> p t c", t=PACK)
-        mass_right = keep.tile([P, T - LEFT], F32, name="mass_right")
-        nc.sync.dma_start(mass_right[:], mass_rows[:, 0, LEFT:])
+        mass_first = keep.tile([P, T - LEFT], F32, name="mass_first")
+        nc.sync.dma_start(mass_first[:], mass_rows[:, 0, LEFT:])
 
         k_scales = keep.tile([P, T], U8, name="k_scales", tag="rest")
         nc.vector.memset(k_scales[:].bitcast(I32), 0)
@@ -61,9 +61,10 @@ def tile_attend_evictscores_pl_kernel(tc, query, keys_words, keys_scales, mass, 
 
         ident = keep.tile([P, P], F32, name="ident")
         make_identity(nc, ident[:])
-        windows = [keep.tile([P, T], F32, name="window%d" % i) for i in range(WINDOWS - 1)]
-        for window in windows:
+        windows = [keep.tile([P, T], F32, name="window%d" % i) for i in range(WINDOWS)]
+        for window in windows[:-1]:
             nc.vector.memset(window[:], 0.0)
+        nc.gpsimd.memset(windows[-1][:], 0.0)
 
         q_bf = keep.tile([P, PACK, P * PACK], BF16, name="q_bf", align_bytes=64)
         q_src = q_raw[:].rearrange("p j (m t) -> p t m j", t=PACK)
@@ -84,29 +85,38 @@ def tile_attend_evictscores_pl_kernel(tc, query, keys_words, keys_scales, mass, 
         nc.vector.tensor_copy(kg_words[:], k_words[:].indirect(slots[:]))
         quantise(1, 2)
         quantise(2, 4)
-        windows.append(keep.tile([P, T], F32, name="window_late", tag="words"))
-        nc.gpsimd.memset(windows[-1][:], 0.0)
 
-        early = keep.tile([P, T + 8], F32, name="early", tag="rest")
-        mass_left = early[:, :LEFT]
-        credit_spread = early[:, LEFT:T]
-        dec_cols = early[:, T : T + PACK]
+        early = keep.tile([P, 2 * T - LEFT + 8], F32, name="early", tag="rest")
+        late = keep.tile([P, 2 * T + LEFT], F32, name="late", tag="first")
+        credit_spread = early[:, : T - LEFT]
+        dec_cols = early[:, 2 * T - LEFT : 2 * T - LEFT + PACK]
+        mass_left = [early[:, T - LEFT : T], late[:, :LEFT], late[:, LEFT : 2 * LEFT], late[:, LEFT + T : 2 * LEFT + T]]
+        mass_right = [mass_first[:], early[:, T : 2 * T - LEFT], late[:, 2 * LEFT : LEFT + T], late[:, 2 * LEFT + T :]]
         nc.sync.dma_start(dec_cols, dec.rearrange("(p t) o -> p (t o)", t=PACK))
         nc.sync.dma_start(credit_spread, credit[0, LEFT:].partition_broadcast(P))
-        nc.sync.dma_start(mass_left, mass_rows[:, 0, :LEFT])
-        mass_rest = keep.tile([P, PACK - 1, T], F32, name="mass_rest", tag="first")
-        for t in range(1, PACK):
-            nc.sync.dma_start(mass_rest[:, t - 1, :], mass_rows[:, t, :])
+        nc.sync.dma_start(mass_right[1], mass_rows[:, 1, LEFT:])
+        nc.sync.dma_start(mass_left[0], mass_rows[:, 0, :LEFT])
+        nc.sync.dma_start(mass_left[1], mass_rows[:, 1, :LEFT])
+        nc.sync.dma_start(mass_right[3], mass_rows[:, 3, LEFT:])
+        nc.sync.dma_start(late[:, LEFT : LEFT + T], mass_rows[:, 2, :])
+        nc.sync.dma_start(mass_left[3], mass_rows[:, 3, :LEFT])
 
         def mass_cols(t, lo, hi):
-            if t > 0:
-                return mass_rest[:, t - 1, lo:hi]
-            return mass_left[:, lo:hi] if hi <= LEFT else mass_right[:, lo - LEFT : hi - LEFT]
+            if hi <= LEFT:
+                return mass_left[t][:, lo:hi]
+            if lo >= LEFT:
+                return mass_right[t][:, lo - LEFT : hi - LEFT]
+            return late[:, LEFT + lo : LEFT + hi]
 
         credit_turned = bank("credit_turned", 3)
         nc.tensor.transpose(credit_turned[:, :P], credit_rows[:], ident[:])
         credit_cols = keep.tile([P, LEFT // P], F32, name="credit_cols")
         nc.scalar.copy(credit_cols[:], credit_turned[:, : LEFT // P])
+
+        spread = [bank("spread", 6 + c) for c in range(LEFT // CHUNK)]
+        for k in range(LEFT // P):
+            c, b = divmod(k, BLOCKS)
+            nc.tensor.transpose(spread[c][:, b * P : (b + 1) * P], credit_cols[:, k : k + 1].to_broadcast([P, P]), ident[:])
 
         neg_max = keep.tile([P, PACK], F32, name="neg_max")
         sums = keep.tile([P, PACK], F32, name="sums")
@@ -152,13 +162,15 @@ def tile_attend_evictscores_pl_kernel(tc, query, keys_words, keys_scales, mass, 
         exponentiate(1)
         normalise(0)
         invert(1, 2)
+        decay_on_scalar(0)
         exponentiate(2)
         exponentiate(3)
         normalise(1)
-        decay_on_scalar(0)
         invert(2, 4)
         normalise(2)
         normalise(3)
+        for t in (1, 3, 2):
+            decay_on_scalar(t)
 
         def scatter(t):
             nc.vector.tensor_copy(windows[t % WINDOWS][:].indirect(slots[:]), weights[t][:])
@@ -174,8 +186,7 @@ def tile_attend_evictscores_pl_kernel(tc, query, keys_words, keys_scales, mass, 
             nc.gpsimd.tensor_tensor(updated[t][:, LEFT:], decayed[t][:, LEFT:], credit_spread, ALU.subtract)
 
         def add_right(t):
-            engine = nc.vector if t == PACK - 1 else nc.gpsimd
-            engine.tensor_tensor(updated[t][:, LEFT:], updated[t][:, LEFT:], windows[t % WINDOWS][:, LEFT:], ALU.add)
+            nc.gpsimd.tensor_tensor(updated[t][:, LEFT:], updated[t][:, LEFT:], windows[t % WINDOWS][:, LEFT:], ALU.add)
 
         def turn(n, t, c):
             cols = slice(c * CHUNK, (c + 1) * CHUNK)
@@ -197,7 +208,7 @@ def tile_attend_evictscores_pl_kernel(tc, query, keys_words, keys_scales, mass, 
             return owed
 
         def turn_back(n, owed):
-            upright = bank("upright", (6, 7, 0, 1, 2)[n % 5])
+            upright = bank("upright", n % 3)
             for block in blocks:
                 nc.tensor.transpose(upright[:, block], owed[:, block], ident[:])
             return upright
@@ -209,34 +220,39 @@ def tile_attend_evictscores_pl_kernel(tc, query, keys_words, keys_scales, mass, 
             else:
                 nc.vector.scalar_tensor_tensor(updated[t][:, cols], mass_cols(t, c * CHUNK, (c + 1) * CHUNK), dec_cols[:, t : t + 1], upright[:], ALU.mult, ALU.subtract)
 
+        def update_last():
+            t = PACK - 1
+            for c in range(LEFT // CHUNK):
+                cols = slice(c * CHUNK, (c + 1) * CHUNK)
+                nc.vector.scalar_tensor_tensor(updated[t][:, cols], mass_left[t][:, cols], dec_cols[:, t : t + 1], spread[c][:], ALU.mult, ALU.subtract)
+            nc.vector.tensor_tensor(updated[t][:, :LEFT], updated[t][:, :LEFT], windows[t % WINDOWS][:, :LEFT], ALU.add)
+            nc.vector.tensor_tensor(updated[t][:, LEFT:], updated[t][:, LEFT:], windows[t % WINDOWS][:, LEFT:], ALU.add)
+
         def look_up(t):
             nc.vector.tensor_copy(picked[:, t, :], updated[t][:].indirect(cands[:]))
-            doubled = keep.tile([P, J], F32, name="doubled%d" % t)
-            nc.scalar.activation(doubled[:], picked[:, t, :], ACT.Copy, scale=2.0)
-            nc.sync.dma_start(out_rows[:, t, :], doubled[:])
+
+        def hand_out(lo, doubled):
+            nc.scalar.activation(doubled, picked[:, lo : lo + 2, :], ACT.Copy, scale=2.0)
+            nc.sync.dma_start(out_rows[:, lo : lo + 2, :], doubled)
 
         for t in range(WINDOWS):
             scatter(t)
         charge_right(0)
         charge_right(1)
-        work = [(t, c) for t in range(PACK) for c in reversed(range(LEFT // CHUNK))]
+        work = [(t, c) for t in range(PACK - 1) for c in reversed(range(LEFT // CHUNK))]
         turned_of, owed_of, upright_of = {}, {}, {}
         for step in range(len(work) + 3):
             if step < len(work):
                 t, c = work[step]
                 turned_of[step] = turn(step, t, c)
                 if c == 0:
-                    if t == 0:
-                        decay_on_scalar(1)
-                    if t == 1:
-                        decay_on_scalar(2)
-                        decay_on_scalar(3)
                     add_right(t)
-                    if t == 1:
-                        charge_right(2)
-                        charge_right(3)
+                    if t < 2:
+                        charge_right(PACK - 1 - t)
                     if t + WINDOWS < PACK:
                         scatter(t + WINDOWS)
+                    if t == 1:
+                        update_last()
             n = step - 1
             if 0 <= n < len(work):
                 owed_of[n] = charge_left(work[n][1], turned_of[n])
@@ -248,7 +264,13 @@ def tile_attend_evictscores_pl_kernel(tc, query, keys_words, keys_scales, mass, 
                 t, c = work[n]
                 finish(t, c, upright_of[n])
                 if c == 0:
+                    if t == PACK - 2:
+                        look_up(PACK - 1)
                     look_up(t)
+
+        hand_out(0, owed_of[len(work) - 1][:].rearrange("p (t j) -> p t j", t=2))
+        doubled = keep.tile([P, 2, J], F32, name="doubled")
+        hand_out(2, doubled[:])
 
         y_bf = keep.tile([P, J * PACK], BF16, name="y_bf", align_bytes=64)
         nc.vector.tensor_scalar(

@@ -1,3 +1,4 @@
+import itertools
 from contextlib import ExitStack
 
 import concourse.mybir as mybir
@@ -19,12 +20,19 @@ AX = mybir.AxisListType
 
 P = 128
 PACK = 4
+LAST = PACK - 1
+QUADRANTS = 4
 CHUNK = 512
 BLOCKS = CHUNK // P
-LEFT = 1024
 WINDOWS = 3
-VECTOR_CHUNKS = (0, 0, 0, 2)
-GPSIMD_DECAYS = (0, 1,)
+
+LEFT = (T // 2, 3 * T // 4, 3 * T // 4, T // 2)
+SPREAD_FROM = min(LEFT)
+VECTOR_CHUNKS = (0, 0, 1)
+
+SCORE_BANKS = (0, 1, 2)
+TURN_BANKS = (6, 7, 3)
+SPREAD_BANKS = (4, 5)
 
 
 def tile_attend_evictscores_pl_kernel(tc, query, keys_words, keys_scales, mass, dec, credit, offs, offs2, out_0, out_1, out_2):
@@ -34,30 +42,30 @@ def tile_attend_evictscores_pl_kernel(tc, query, keys_words, keys_scales, mass, 
         ring = ctx.enter_context(tc.tile_pool(name="ring", bufs=4))
         psum = ctx.enter_context(tc.psum_pool(name="psum", bufs=1))
 
-        def bank(name, b):
-            return psum.tile([P, CHUNK], F32, name=name, tag="bank%d" % b)
+        def bank(name, number):
+            return psum.tile([P, CHUNK], F32, name=name, tag="bank%d" % number)
 
         slots = keep.tile([P, I // 16], U16, name="slots")
         nc.sync.dma_start(slots[:], offs)
         cands = keep.tile([P, J // 16], U16, name="cands")
         nc.sync.dma_start(cands[:], offs2)
-        q_raw = keep.tile([P, PACK, Q], F32, name="q_raw", tag="first")
+        q_raw = keep.tile([P, PACK, Q], F32, name="q_raw", tag="query_then_mass")
         nc.sync.dma_start(q_raw[:], query.rearrange("(p j) c -> p j c", j=PACK))
         k_words = keep.tile([P, T], U32, name="k_words")
         nc.sync.dma_start(k_words[:].bitcast(I32), keys_words[0].rearrange("p c r -> p (c r)").bitcast(I32))
 
         mass_rows = mass.rearrange("(p t) c -> p t c", t=PACK)
-        mass_first = keep.tile([P, T - LEFT], F32, name="mass_first")
-        nc.sync.dma_start(mass_first[:], mass_rows[:, 0, LEFT:])
-
-        k_scales = keep.tile([P, T], U8, name="k_scales", tag="rest")
-        nc.vector.memset(k_scales[:].bitcast(I32), 0)
-        for quad in range(4):
-            nc.scalar.dma_start(k_scales[32 * quad : 32 * quad + 4, :].bitcast(I32), keys_scales[0, 4 * quad : 4 * quad + 4, :].bitcast(I32))
+        right_0 = keep.tile([P, T - LEFT[0]], F32, name="right_0")
+        nc.sync.dma_start(right_0[:], mass_rows[:, 0, LEFT[0] :])
 
         credit_rows = keep.tile([P, P], F32, name="credit_rows")
         nc.gpsimd.memset(credit_rows[:], 0.0)
-        nc.scalar.dma_start(credit_rows[0 : LEFT // P, :], credit[:, :LEFT].rearrange("o (b m) -> (o b) m", m=P))
+        nc.scalar.dma_start(credit_rows[0 : T // P, :], credit.rearrange("o (b m) -> (o b) m", m=P))
+
+        k_scales = keep.tile([P, T], U8, name="k_scales", tag="scales_then_mass")
+        nc.vector.memset(k_scales[:].bitcast(I32), 0)
+        for quad in range(QUADRANTS):
+            nc.scalar.dma_start(k_scales[32 * quad : 32 * quad + 4, :].bitcast(I32), keys_scales[0, 4 * quad : 4 * quad + 4, :].bitcast(I32))
 
         ident = keep.tile([P, P], F32, name="ident")
         make_identity(nc, ident[:])
@@ -66,7 +74,7 @@ def tile_attend_evictscores_pl_kernel(tc, query, keys_words, keys_scales, mass, 
             nc.vector.memset(window[:], 0.0)
         nc.gpsimd.memset(windows[-1][:], 0.0)
 
-        q_bf = keep.tile([P, PACK, P * PACK], BF16, name="q_bf", align_bytes=64)
+        q_bf = keep.tile([P, PACK, P * PACK], BF16, name="q_bf", tag="rounded_then_decayed", align_bytes=64)
         q_src = q_raw[:].rearrange("p j (m t) -> p t m j", t=PACK)
         q_words = keep.tile([P, Q], U32, name="q_words", align_bytes=64)
         q_scales = keep.tile([P, Q], U8, name="q_scales", align_bytes=64)
@@ -84,39 +92,45 @@ def tile_attend_evictscores_pl_kernel(tc, query, keys_words, keys_scales, mass, 
         kg_words = keep.tile([P, I], U32, name="kg_words", align_bytes=64)
         nc.vector.tensor_copy(kg_words[:], k_words[:].indirect(slots[:]))
         quantise(1, 2)
-        quantise(2, 4)
+        quantise(2, PACK)
 
-        early = keep.tile([P, 2 * T - LEFT + 8], F32, name="early", tag="rest")
-        late = keep.tile([P, 2 * T + LEFT], F32, name="late", tag="first")
-        credit_spread = early[:, : T - LEFT]
-        dec_cols = early[:, 2 * T - LEFT : 2 * T - LEFT + PACK]
-        mass_left = [early[:, T - LEFT : T], late[:, :LEFT], late[:, LEFT : 2 * LEFT], late[:, LEFT + T : 2 * LEFT + T]]
-        mass_right = [mass_first[:], early[:, T : 2 * T - LEFT], late[:, 2 * LEFT : LEFT + T], late[:, 2 * LEFT + T :]]
+        def carve(tile, widths):
+            ends = list(itertools.accumulate(widths))
+            return [tile[:, end - width : end] for end, width in zip(ends, widths)]
+
+        early_widths = [T - LEFT[1], LEFT[0], 2 * PACK]
+        early = keep.tile([P, sum(early_widths)], F32, name="early", tag="scales_then_mass")
+        right_1, left_0, dec_padded = carve(early, early_widths)
+        dec_cols = dec_padded[:, :PACK]
+        late_widths = [LEFT[1], T - LEFT[3], T, LEFT[3]]
+        late = keep.tile([P, sum(late_widths)], F32, name="late", tag="query_then_mass")
+        left_1, right_3, whole_2, left_3 = carve(late, late_widths)
         nc.sync.dma_start(dec_cols, dec.rearrange("(p t) o -> p (t o)", t=PACK))
-        nc.sync.dma_start(credit_spread, credit[0, LEFT:].partition_broadcast(P))
-        nc.sync.dma_start(mass_right[1], mass_rows[:, 1, LEFT:])
-        nc.sync.dma_start(mass_left[0], mass_rows[:, 0, :LEFT])
-        nc.sync.dma_start(mass_left[1], mass_rows[:, 1, :LEFT])
-        nc.sync.dma_start(mass_right[3], mass_rows[:, 3, LEFT:])
-        nc.sync.dma_start(late[:, LEFT : LEFT + T], mass_rows[:, 2, :])
-        nc.sync.dma_start(mass_left[3], mass_rows[:, 3, :LEFT])
+        nc.sync.dma_start(right_1, mass_rows[:, 1, LEFT[1] :])
+        nc.sync.dma_start(left_0, mass_rows[:, 0, : LEFT[0]])
+        nc.sync.dma_start(left_1, mass_rows[:, 1, : LEFT[1]])
+        nc.sync.dma_start(right_3, mass_rows[:, 3, LEFT[3] :])
+        nc.sync.dma_start(whole_2, mass_rows[:, 2, :])
+        nc.sync.dma_start(left_3, mass_rows[:, 3, : LEFT[3]])
+        mass_left = [left_0, left_1, whole_2[:, : LEFT[2]], left_3]
+        mass_right = [right_0[:], right_1, whole_2[:, LEFT[2] :], right_3]
 
-        def mass_cols(t, lo, hi):
-            if hi <= LEFT:
-                return mass_left[t][:, lo:hi]
-            if lo >= LEFT:
-                return mass_right[t][:, lo - LEFT : hi - LEFT]
-            return late[:, LEFT + lo : LEFT + hi]
-
-        credit_turned = bank("credit_turned", 3)
+        credit_turned = bank("credit_turned", TURN_BANKS[-1])
         nc.tensor.transpose(credit_turned[:, :P], credit_rows[:], ident[:])
-        credit_cols = keep.tile([P, LEFT // P], F32, name="credit_cols")
-        nc.scalar.copy(credit_cols[:], credit_turned[:, : LEFT // P])
+        credit_cols = keep.tile([P, T // P], F32, name="credit_cols")
+        nc.scalar.copy(credit_cols[:], credit_turned[:, : T // P])
 
-        spread = [bank("spread", 6 + c) for c in range(LEFT // CHUNK)]
-        for k in range(LEFT // P):
-            c, b = divmod(k, BLOCKS)
-            nc.tensor.transpose(spread[c][:, b * P : (b + 1) * P], credit_cols[:, k : k + 1].to_broadcast([P, P]), ident[:])
+        def spread_credit(c):
+            spread = bank("spread", SPREAD_BANKS[c % len(SPREAD_BANKS)])
+            for b in range(BLOCKS):
+                k = c * BLOCKS + b
+                nc.tensor.transpose(spread[:, b * P : (b + 1) * P], credit_cols[:, k : k + 1].to_broadcast([P, P]), ident[:])
+            return spread
+
+        credit_sbuf = keep.tile([P, T - SPREAD_FROM], F32, name="credit_sbuf")
+        for c in range(SPREAD_FROM // CHUNK, T // CHUNK):
+            nc.scalar.copy(credit_sbuf[:, c * CHUNK - SPREAD_FROM : (c + 1) * CHUNK - SPREAD_FROM], spread_credit(c)[:])
+        credit_psum = [spread_credit(c) for c in range(LEFT[LAST] // CHUNK)]
 
         neg_max = keep.tile([P, PACK], F32, name="neg_max")
         sums = keep.tile([P, PACK], F32, name="sums")
@@ -127,7 +141,7 @@ def tile_attend_evictscores_pl_kernel(tc, query, keys_words, keys_scales, mass, 
 
         def exponentiate(t):
             heads = slice(t * P, (t + 1) * P)
-            scores = bank("scores", t % 3)
+            scores = bank("scores", SCORE_BANKS[t % len(SCORE_BANKS)])
             nc.tensor.matmul_mx(
                 out=scores[:],
                 lhsT=q_words[:, heads].bitcast(FP8X4),
@@ -143,19 +157,23 @@ def tile_attend_evictscores_pl_kernel(tc, query, keys_words, keys_scales, mass, 
         def invert(lo, hi):
             nc.vector.reciprocal(inverses[:, lo:hi], sums[:, lo:hi])
             if lo == 0:
-                nc.vector.tensor_scalar(gains[:, lo:hi], inverses[:, lo:hi], float(I), None, ALU.mult)
+                nc.vector.tensor_scalar(inverses[:, lo:hi], inverses[:, lo:hi], float(I), None, ALU.mult, ALU.add, accum_out=gains[:, lo:hi])
             else:
                 nc.scalar.activation(gains[:, lo:hi], inverses[:, lo:hi], ACT.Copy, scale=float(I))
 
         def normalise(t):
             nc.scalar.activation(weights[t][:], probs[t][:], ACT.Copy, scale=gains[:, t : t + 1])
 
-        decayed = [keep.tile([P, T], F32, name="decayed%d" % t) for t in range(PACK)]
+        decayed_left = [keep.tile([P, LEFT[t]], F32, name="decayed_left%d" % t) for t in range(LAST)]
+        decayed_right = [keep.tile([P, T - LEFT[0]], F32, name="decayed_right0", tag="rounded_then_decayed", align_bytes=64)]
+        decayed_right.extend([keep.tile([P, T - LEFT[t]], F32, name="decayed_right%d" % t) for t in range(1, PACK)])
 
         def decay_on_scalar(t):
-            lo = VECTOR_CHUNKS[t] * CHUNK
-            hi = LEFT if t in GPSIMD_DECAYS else T
-            nc.scalar.activation(decayed[t][:, lo:hi], mass_cols(t, lo, hi), ACT.Copy, scale=dec_cols[:, t : t + 1])
+            if t < LAST:
+                lo = VECTOR_CHUNKS[t] * CHUNK
+                nc.scalar.activation(decayed_left[t][:, lo:], mass_left[t][:, lo:], ACT.Copy, scale=dec_cols[:, t : t + 1])
+            else:
+                nc.scalar.activation(decayed_right[t][:], mass_right[t], ACT.Copy, scale=dec_cols[:, t : t + 1])
 
         exponentiate(0)
         invert(0, 1)
@@ -166,10 +184,10 @@ def tile_attend_evictscores_pl_kernel(tc, query, keys_words, keys_scales, mass, 
         exponentiate(2)
         exponentiate(3)
         normalise(1)
-        invert(2, 4)
+        invert(2, PACK)
         normalise(2)
         normalise(3)
-        for t in (1, 3, 2):
+        for t in (1, LAST, 2):
             decay_on_scalar(t)
 
         def scatter(t):
@@ -181,17 +199,17 @@ def tile_attend_evictscores_pl_kernel(tc, query, keys_words, keys_scales, mass, 
         blocks = [slice(b * P, (b + 1) * P) for b in range(BLOCKS)]
 
         def charge_right(t):
-            if t in GPSIMD_DECAYS:
-                nc.gpsimd.tensor_scalar(decayed[t][:, LEFT:], mass_cols(t, LEFT, T), dec_cols[:, t : t + 1], 0.0, ALU.mult, ALU.add)
-            nc.gpsimd.tensor_tensor(updated[t][:, LEFT:], decayed[t][:, LEFT:], credit_spread, ALU.subtract)
+            if t < LAST:
+                nc.gpsimd.tensor_scalar(decayed_right[t][:], mass_right[t], dec_cols[:, t : t + 1], 0.0, ALU.mult, ALU.add)
+            nc.gpsimd.tensor_tensor(updated[t][:, LEFT[t] :], decayed_right[t][:], credit_sbuf[:, LEFT[t] - SPREAD_FROM :], ALU.subtract)
 
         def add_right(t):
-            nc.gpsimd.tensor_tensor(updated[t][:, LEFT:], updated[t][:, LEFT:], windows[t % WINDOWS][:, LEFT:], ALU.add)
+            nc.gpsimd.tensor_tensor(updated[t][:, LEFT[t] :], updated[t][:, LEFT[t] :], windows[t % WINDOWS][:, LEFT[t] :], ALU.add)
 
         def turn(n, t, c):
             cols = slice(c * CHUNK, (c + 1) * CHUNK)
-            turned = bank("turned", 3 + n % 3)
-            terms = [decayed[t][:, cols]] if c >= VECTOR_CHUNKS[t] else []
+            turned = bank("turned", TURN_BANKS[n % len(TURN_BANKS)])
+            terms = [decayed_left[t][:, cols]] if c >= VECTOR_CHUNKS[t] else []
             terms.append(windows[t % WINDOWS][:, cols])
             for i, term in enumerate(terms):
                 for b, block in enumerate(blocks):
@@ -208,7 +226,7 @@ def tile_attend_evictscores_pl_kernel(tc, query, keys_words, keys_scales, mass, 
             return owed
 
         def turn_back(n, owed):
-            upright = bank("upright", n % 3)
+            upright = bank("upright", SCORE_BANKS[n % len(SCORE_BANKS)])
             for block in blocks:
                 nc.tensor.transpose(upright[:, block], owed[:, block], ident[:])
             return upright
@@ -218,15 +236,14 @@ def tile_attend_evictscores_pl_kernel(tc, query, keys_words, keys_scales, mass, 
             if c >= VECTOR_CHUNKS[t]:
                 nc.scalar.activation(updated[t][:, cols], upright[:], ACT.Copy, scale=-1.0)
             else:
-                nc.vector.scalar_tensor_tensor(updated[t][:, cols], mass_cols(t, c * CHUNK, (c + 1) * CHUNK), dec_cols[:, t : t + 1], upright[:], ALU.mult, ALU.subtract)
+                nc.vector.scalar_tensor_tensor(updated[t][:, cols], mass_left[t][:, cols], dec_cols[:, t : t + 1], upright[:], ALU.mult, ALU.subtract)
 
         def update_last():
-            t = PACK - 1
-            for c in range(LEFT // CHUNK):
+            for c, spread in enumerate(credit_psum):
                 cols = slice(c * CHUNK, (c + 1) * CHUNK)
-                nc.vector.scalar_tensor_tensor(updated[t][:, cols], mass_left[t][:, cols], dec_cols[:, t : t + 1], spread[c][:], ALU.mult, ALU.subtract)
-            nc.vector.tensor_tensor(updated[t][:, :LEFT], updated[t][:, :LEFT], windows[t % WINDOWS][:, :LEFT], ALU.add)
-            nc.vector.tensor_tensor(updated[t][:, LEFT:], updated[t][:, LEFT:], windows[t % WINDOWS][:, LEFT:], ALU.add)
+                nc.vector.scalar_tensor_tensor(updated[LAST][:, cols], mass_left[LAST][:, cols], dec_cols[:, LAST:], spread[:], ALU.mult, ALU.subtract)
+            for cols in (slice(0, LEFT[LAST]), slice(LEFT[LAST], T)):
+                nc.vector.tensor_tensor(updated[LAST][:, cols], updated[LAST][:, cols], windows[LAST % WINDOWS][:, cols], ALU.add)
 
         def look_up(t):
             nc.vector.tensor_copy(picked[:, t, :], updated[t][:].indirect(cands[:]))
@@ -239,7 +256,7 @@ def tile_attend_evictscores_pl_kernel(tc, query, keys_words, keys_scales, mass, 
             scatter(t)
         charge_right(0)
         charge_right(1)
-        work = [(t, c) for t in range(PACK - 1) for c in reversed(range(LEFT // CHUNK))]
+        work = [(t, c) for t in range(LAST) for c in reversed(range(LEFT[t] // CHUNK))]
         turned_of, owed_of, upright_of = {}, {}, {}
         for step in range(len(work) + 3):
             if step < len(work):
@@ -247,11 +264,11 @@ def tile_attend_evictscores_pl_kernel(tc, query, keys_words, keys_scales, mass, 
                 turned_of[step] = turn(step, t, c)
                 if c == 0:
                     add_right(t)
-                    if t < 2:
-                        charge_right(PACK - 1 - t)
-                    if t + WINDOWS < PACK:
-                        scatter(t + WINDOWS)
-                    if t == 1:
+                    if t < LAST - t:
+                        charge_right(LAST - t)
+                    if t + WINDOWS == LAST:
+                        scatter(LAST)
+                    if t + WINDOWS == LAST + 1:
                         update_last()
             n = step - 1
             if 0 <= n < len(work):
@@ -264,8 +281,8 @@ def tile_attend_evictscores_pl_kernel(tc, query, keys_words, keys_scales, mass, 
                 t, c = work[n]
                 finish(t, c, upright_of[n])
                 if c == 0:
-                    if t == PACK - 2:
-                        look_up(PACK - 1)
+                    if n == len(work) - 1:
+                        look_up(LAST)
                     look_up(t)
 
         hand_out(0, owed_of[len(work) - 1][:].rearrange("p (t j) -> p t j", t=2))
@@ -284,6 +301,6 @@ def tile_attend_evictscores_pl_kernel(tc, query, keys_words, keys_scales, mass, 
         y_scales = keep.tile([P, J], U8, name="y_scales", align_bytes=64)
         nc.vector.quantize_mx(out=y_words[:].bitcast(FP8X4), scales=y_scales[:], in_=y_bf[:])
         nc.sync.dma_start(out_1[0].rearrange("p c r -> p (c r)").bitcast(I32), y_words[:].bitcast(I32))
-        for quad in range(4):
+        for quad in range(QUADRANTS):
             queue = nc.scalar if quad % 2 == 0 else nc.sync
             queue.dma_start(out_2[0, 4 * quad : 4 * quad + 4, :].bitcast(I32), y_scales[32 * quad : 32 * quad + 4, :].bitcast(I32))

import itertools
from contextlib import ExitStack

import concourse.mybir as mybir
from concourse.masks import make_identity

D, T, I, J, Q = 512, 2048, 512, 256, 512
FLOPS = 2 * D * Q * I

F32 = mybir.dt.float32
BF16 = mybir.dt.bfloat16
I32 = mybir.dt.int32
U32 = mybir.dt.uint32
U16 = mybir.dt.uint16
U8 = mybir.dt.uint8
FP8X4 = mybir.dt.float8_e4m3fn_x4
ACT = mybir.ActivationFunctionType
ALU = mybir.AluOpType
AX = mybir.AxisListType

P = 128
PACK = 4
LAST = PACK - 1
QUADRANTS = 4
CHUNK = 512
BLOCKS = CHUNK // P
WINDOWS = 3

LEFT = (T // 2, 3 * T // 4, 3 * T // 4, T // 2)
SPREAD_FROM = min(LEFT)
VECTOR_CHUNKS = (0, 0, 1)

SCORE_BANKS = (0, 1, 2)
TURN_BANKS = (6, 7, 3)
SPREAD_BANKS = (4, 5)


def tile_attend_evictscores_pl_kernel(tc, query, keys_words, keys_scales, mass, dec, credit, offs, offs2, out_0, out_1, out_2):
    nc = tc.nc
    with ExitStack() as ctx:
        keep = ctx.enter_context(tc.tile_pool(name="keep", bufs=1))
        ring = ctx.enter_context(tc.tile_pool(name="ring", bufs=4))
        psum = ctx.enter_context(tc.psum_pool(name="psum", bufs=1))

        def bank(name, number):
            return psum.tile([P, CHUNK], F32, name=name, tag="bank%d" % number)

        slots = keep.tile([P, I // 16], U16, name="slots")
        nc.sync.dma_start(slots[:], offs)
        cands = keep.tile([P, J // 16], U16, name="cands")
        nc.sync.dma_start(cands[:], offs2)
        q_raw = keep.tile([P, PACK, Q], F32, name="q_raw", tag="query_then_mass")
        nc.sync.dma_start(q_raw[:], query.rearrange("(p j) c -> p j c", j=PACK))
        k_words = keep.tile([P, T], U32, name="k_words")
        nc.sync.dma_start(k_words[:].bitcast(I32), keys_words[0].rearrange("p c r -> p (c r)").bitcast(I32))

        mass_rows = mass.rearrange("(p t) c -> p t c", t=PACK)
        right_0 = keep.tile([P, T - LEFT[0]], F32, name="right_0")
        nc.sync.dma_start(right_0[:], mass_rows[:, 0, LEFT[0] :])

        credit_rows = keep.tile([P, P], F32, name="credit_rows")
        nc.gpsimd.memset(credit_rows[:], 0.0)
        nc.scalar.dma_start(credit_rows[0 : T // P, :], credit.rearrange("o (b m) -> (o b) m", m=P))

        k_scales = keep.tile([P, T], U8, name="k_scales", tag="scales_then_mass")
        nc.vector.memset(k_scales[:].bitcast(I32), 0)
        for quad in range(QUADRANTS):
            nc.scalar.dma_start(k_scales[32 * quad : 32 * quad + 4, :].bitcast(I32), keys_scales[0, 4 * quad : 4 * quad + 4, :].bitcast(I32))

        ident = keep.tile([P, P], F32, name="ident")
        make_identity(nc, ident[:])
        windows = [keep.tile([P, T], F32, name="window%d" % i) for i in range(WINDOWS)]
        for window in windows[:-1]:
            nc.vector.memset(window[:], 0.0)
        nc.gpsimd.memset(windows[-1][:], 0.0)

        q_bf = keep.tile([P, PACK, P * PACK], BF16, name="q_bf", tag="rounded_then_decayed", align_bytes=64)
        q_src = q_raw[:].rearrange("p j (m t) -> p t m j", t=PACK)
        q_words = keep.tile([P, Q], U32, name="q_words", align_bytes=64)
        q_scales = keep.tile([P, Q], U8, name="q_scales", align_bytes=64)

        def quantise(lo, hi):
            heads = slice(lo * P, hi * P)
            nc.vector.quantize_mx(out=q_words[:, heads].bitcast(FP8X4), scales=q_scales[:, heads], in_=q_bf[:, lo:hi, :].rearrange("p t k -> p (t k)"))

        nc.vector.tensor_copy(q_bf[:, 0, :].rearrange("p (m j) -> p m j", j=PACK), q_src[:, 0])
        for t in range(1, PACK):
            nc.scalar.copy(q_bf[:, t, :].rearrange("p (m j) -> p m j", j=PACK), q_src[:, t])
        quantise(0, 1)
        kg_scales = keep.tile([P, I], U8, name="kg_scales", align_bytes=64)
        nc.vector.tensor_copy(kg_scales[:], k_scales[:].indirect(slots[:]))
        kg_words = keep.tile([P, I], U32, name="kg_words", align_bytes=64)
        nc.vector.tensor_copy(kg_words[:], k_words[:].indirect(slots[:]))
        quantise(1, 2)
        quantise(2, PACK)

        def carve(tile, widths):
            ends = list(itertools.accumulate(widths))
            return [tile[:, end - width : end] for end, width in zip(ends, widths)]

        early_widths = [T - LEFT[1], LEFT[0], 2 * PACK]
        early = keep.tile([P, sum(early_widths)], F32, name="early", tag="scales_then_mass")
        right_1, left_0, dec_padded = carve(early, early_widths)
        dec_cols = dec_padded[:, :PACK]
        late_widths = [LEFT[1], T - LEFT[3], T, LEFT[3]]
        late = keep.tile([P, sum(late_widths)], F32, name="late", tag="query_then_mass")
        left_1, right_3, whole_2, left_3 = carve(late, late_widths)
        nc.sync.dma_start(dec_cols, dec.rearrange("(p t) o -> p (t o)", t=PACK))
        nc.sync.dma_start(right_1, mass_rows[:, 1, LEFT[1] :])
        nc.sync.dma_start(left_0, mass_rows[:, 0, : LEFT[0]])
        nc.sync.dma_start(left_1, mass_rows[:, 1, : LEFT[1]])
        nc.sync.dma_start(right_3, mass_rows[:, 3, LEFT[3] :])
        nc.sync.dma_start(whole_2, mass_rows[:, 2, :])
        nc.sync.dma_start(left_3, mass_rows[:, 3, : LEFT[3]])
        mass_left = [left_0, left_1, whole_2[:, : LEFT[2]], left_3]
        mass_right = [right_0[:], right_1, whole_2[:, LEFT[2] :], right_3]

        credit_turned = bank("credit_turned", TURN_BANKS[-1])
        nc.tensor.transpose(credit_turned[:, :P], credit_rows[:], ident[:])
        credit_cols = keep.tile([P, T // P], F32, name="credit_cols")
        nc.scalar.copy(credit_cols[:], credit_turned[:, : T // P])

        def spread_credit(c):
            spread = bank("spread", SPREAD_BANKS[c % len(SPREAD_BANKS)])
            for b in range(BLOCKS):
                k = c * BLOCKS + b
                nc.tensor.transpose(spread[:, b * P : (b + 1) * P], credit_cols[:, k : k + 1].to_broadcast([P, P]), ident[:])
            return spread

        credit_sbuf = keep.tile([P, T - SPREAD_FROM], F32, name="credit_sbuf")
        for c in range(SPREAD_FROM // CHUNK, T // CHUNK):
            nc.scalar.copy(credit_sbuf[:, c * CHUNK - SPREAD_FROM : (c + 1) * CHUNK - SPREAD_FROM], spread_credit(c)[:])
        credit_psum = [spread_credit(c) for c in range(LEFT[LAST] // CHUNK)]

        neg_max = keep.tile([P, PACK], F32, name="neg_max")
        sums = keep.tile([P, PACK], F32, name="sums")
        inverses = keep.tile([P, PACK], F32, name="inverses")
        gains = keep.tile([P, PACK], F32, name="gains")
        probs = [keep.tile([P, I], F32, name="probs%d" % t) for t in range(PACK)]
        weights = [keep.tile([P, I], F32, name="weights%d" % t) for t in range(PACK)]

        def exponentiate(t):
            heads = slice(t * P, (t + 1) * P)
            scores = bank("scores", SCORE_BANKS[t % len(SCORE_BANKS)])
            nc.tensor.matmul_mx(
                out=scores[:],
                lhsT=q_words[:, heads].bitcast(FP8X4),
                lhsT_scale=q_scales[:, heads],
                rhs=kg_words[:].bitcast(FP8X4),
                rhs_scale=kg_scales[:],
                start=True,
                stop=True,
            )
            nc.vector.tensor_reduce(neg_max[:, t : t + 1], scores[:], AX.X, ALU.max, negate=True)
            nc.scalar.activation(probs[t][:], scores[:], ACT.Exp, bias=neg_max[:, t : t + 1], accum_out=sums[:, t : t + 1])

        def invert(lo, hi):
            nc.vector.reciprocal(inverses[:, lo:hi], sums[:, lo:hi])
            if lo == 0:
                nc.vector.tensor_scalar(inverses[:, lo:hi], inverses[:, lo:hi], float(I), None, ALU.mult, ALU.add, accum_out=gains[:, lo:hi])
            else:
                nc.scalar.activation(gains[:, lo:hi], inverses[:, lo:hi], ACT.Copy, scale=float(I))

        def normalise(t):
            nc.scalar.activation(weights[t][:], probs[t][:], ACT.Copy, scale=gains[:, t : t + 1])

        decayed_left = [keep.tile([P, LEFT[t]], F32, name="decayed_left%d" % t) for t in range(LAST)]
        decayed_right = [keep.tile([P, T - LEFT[0]], F32, name="decayed_right0", tag="rounded_then_decayed", align_bytes=64)]
        decayed_right.extend([keep.tile([P, T - LEFT[t]], F32, name="decayed_right%d" % t) for t in range(1, PACK)])

        def decay_on_scalar(t):
            if t < LAST:
                lo = VECTOR_CHUNKS[t] * CHUNK
                nc.scalar.activation(decayed_left[t][:, lo:], mass_left[t][:, lo:], ACT.Copy, scale=dec_cols[:, t : t + 1])
            else:
                nc.scalar.activation(decayed_right[t][:], mass_right[t], ACT.Copy, scale=dec_cols[:, t : t + 1])

        exponentiate(0)
        invert(0, 1)
        exponentiate(1)
        normalise(0)
        invert(1, 2)
        decay_on_scalar(0)
        exponentiate(2)
        exponentiate(3)
        normalise(1)
        invert(2, PACK)
        normalise(2)
        normalise(3)
        for t in (1, LAST, 2):
            decay_on_scalar(t)

        def scatter(t):
            nc.vector.tensor_copy(windows[t % WINDOWS][:].indirect(slots[:]), weights[t][:])

        updated = [keep.tile([P, T], F32, name="updated%d" % t) for t in range(PACK)]
        picked = keep.tile([P, PACK, J], F32, name="picked")
        out_rows = out_0.rearrange("(p t) j -> p t j", t=PACK)
        blocks = [slice(b * P, (b + 1) * P) for b in range(BLOCKS)]

        def charge_right(t):
            if t < LAST:
                nc.gpsimd.tensor_scalar(decayed_right[t][:], mass_right[t], dec_cols[:, t : t + 1], 0.0, ALU.mult, ALU.add)
            nc.gpsimd.tensor_tensor(updated[t][:, LEFT[t] :], decayed_right[t][:], credit_sbuf[:, LEFT[t] - SPREAD_FROM :], ALU.subtract)

        def add_right(t):
            nc.gpsimd.tensor_tensor(updated[t][:, LEFT[t] :], updated[t][:, LEFT[t] :], windows[t % WINDOWS][:, LEFT[t] :], ALU.add)

        def turn(n, t, c):
            cols = slice(c * CHUNK, (c + 1) * CHUNK)
            turned = bank("turned", TURN_BANKS[n % len(TURN_BANKS)])
            terms = [decayed_left[t][:, cols]] if c >= VECTOR_CHUNKS[t] else []
            terms.append(windows[t % WINDOWS][:, cols])
            for i, term in enumerate(terms):
                for b, block in enumerate(blocks):
                    first = i == 0 and b == 0
                    last = i == len(terms) - 1 and b == BLOCKS - 1
                    nc.tensor.matmul(turned[:, block], term[:, block], ident[:], start=first, stop=last, is_transpose=True)
            return turned

        def charge_left(c, turned):
            owed = ring.tile([P, CHUNK], F32, name="owed")
            for b, block in enumerate(blocks):
                k = c * BLOCKS + b
                nc.scalar.activation(owed[:, block], turned[:, block], ACT.Identity, scale=-1.0, bias=credit_cols[:, k : k + 1])
            return owed

        def turn_back(n, owed):
            upright = bank("upright", SCORE_BANKS[n % len(SCORE_BANKS)])
            for block in blocks:
                nc.tensor.transpose(upright[:, block], owed[:, block], ident[:])
            return upright

        def finish(t, c, upright):
            cols = slice(c * CHUNK, (c + 1) * CHUNK)
            if c >= VECTOR_CHUNKS[t]:
                nc.scalar.activation(updated[t][:, cols], upright[:], ACT.Copy, scale=-1.0)
            else:
                nc.vector.scalar_tensor_tensor(updated[t][:, cols], mass_left[t][:, cols], dec_cols[:, t : t + 1], upright[:], ALU.mult, ALU.subtract)

        def update_last():
            for c, spread in enumerate(credit_psum):
                cols = slice(c * CHUNK, (c + 1) * CHUNK)
                nc.vector.scalar_tensor_tensor(updated[LAST][:, cols], mass_left[LAST][:, cols], dec_cols[:, LAST:], spread[:], ALU.mult, ALU.subtract)
            for cols in (slice(0, LEFT[LAST]), slice(LEFT[LAST], T)):
                nc.vector.tensor_tensor(updated[LAST][:, cols], updated[LAST][:, cols], windows[LAST % WINDOWS][:, cols], ALU.add)

        def look_up(t):
            nc.vector.tensor_copy(picked[:, t, :], updated[t][:].indirect(cands[:]))

        def hand_out(lo, doubled):
            nc.scalar.activation(doubled, picked[:, lo : lo + 2, :], ACT.Copy, scale=2.0)
            nc.sync.dma_start(out_rows[:, lo : lo + 2, :], doubled)

        for t in range(WINDOWS):
            scatter(t)
        charge_right(0)
        charge_right(1)
        work = [(t, c) for t in range(LAST) for c in reversed(range(LEFT[t] // CHUNK))]
        turned_of, owed_of, upright_of = {}, {}, {}
        for step in range(len(work) + 3):
            if step < len(work):
                t, c = work[step]
                turned_of[step] = turn(step, t, c)
                if c == 0:
                    add_right(t)
                    if t < LAST - t:
                        charge_right(LAST - t)
                    if t + WINDOWS == LAST:
                        scatter(LAST)
                    if t + WINDOWS == LAST + 1:
                        update_last()
            n = step - 1
            if 0 <= n < len(work):
                owed_of[n] = charge_left(work[n][1], turned_of[n])
            n = step - 2
            if 0 <= n < len(work):
                upright_of[n] = turn_back(n, owed_of[n])
            n = step - 3
            if 0 <= n < len(work):
                t, c = work[n]
                finish(t, c, upright_of[n])
                if c == 0:
                    if n == len(work) - 1:
                        look_up(LAST)
                    look_up(t)

        hand_out(0, owed_of[len(work) - 1][:].rearrange("p (t j) -> p t j", t=2))
        doubled = keep.tile([P, 2, J], F32, name="doubled")
        hand_out(2, doubled[:])

        y_bf = keep.tile([P, J * PACK], BF16, name="y_bf", align_bytes=64)
        nc.vector.tensor_scalar(
            y_bf[:].rearrange("p (c i t) -> p c t i", i=4, t=PACK),
            picked[:].rearrange("p t (c i) -> p c t i", i=4),
            2.0,
            None,
            ALU.mult,
        )
        y_words = keep.tile([P, J], U32, name="y_words", align_bytes=64)
        y_scales = keep.tile([P, J], U8, name="y_scales", align_bytes=64)
        nc.vector.quantize_mx(out=y_words[:].bitcast(FP8X4), scales=y_scales[:], in_=y_bf[:])
        nc.sync.dma_start(out_1[0].rearrange("p c r -> p (c r)").bitcast(I32), y_words[:].bitcast(I32))
        for quad in range(QUADRANTS):
            queue = nc.scalar if quad % 2 == 0 else nc.sync
            queue.dma_start(out_2[0, 4 * quad : 4 * quad + 4, :].bitcast(I32), y_scales[32 * quad : 32 * quad + 4, :].bitcast(I32))
